import numpy as np
import ml_dtypes

BF16 = ml_dtypes.bfloat16


def bf(x):
    return np.asarray(x, np.float32).astype(BF16)


def f32(x):
    return np.asarray(x, np.float32)


def f64(x):
    return np.asarray(x).astype(np.float64)


def striped(idx):
    return np.tile(idx.reshape(-1, 16).T, (8, 1))


S, K, M, N, D, V = 512, 256, 256, 384, 2, 192


def setup_inputs():
    return {"table": bf(np.random.standard_normal((K, S))), "w": bf(np.random.standard_normal((K, M)) / np.sqrt(D * K)), "b": f32(0.5 * np.random.standard_normal((M, 1))), "offs": striped(np.random.permutation(np.tile(np.arange(S), 2))[:N])}


def reference(table, w, b, offs):
    idx = offs[:16].T.reshape(-1)
    x = f64(table)[:, idx]
    y = f64(w).T @ sum(x[:, t * V : (t + 1) * V] for t in range(D))
    return np.maximum(y + f64(b), 0.0)

@@ -1,0 +1,59 @@
+import concourse.mybir as mybir
+
+P = 128
+K = 256
+M = 256
+S = 512
+V = 192
+NEIGHBOURS = 2
+K_BLOCKS = K // P
+M_BLOCKS = M // P
+PIECE_COLS = V // 16
+
+FLOPS = 2 * K * M * V
+
+BF16 = mybir.dt.bfloat16
+F32 = mybir.dt.float32
+U16 = mybir.dt.uint16
+
+
+def tile_gather_matmul_kernel(tc, table, w, b, offs, out):
+    nc = tc.nc
+    with (
+        tc.tile_pool(name="held", bufs=1) as held,
+        tc.psum_pool(name="psum", bufs=1) as psum,
+    ):
+        table_blocks = [held.tile([P, S], BF16, name="table_block%d" % kb) for kb in range(K_BLOCKS)]
+        w_blocks = [held.tile([P, M], BF16, name="w_block%d" % kb) for kb in range(K_BLOCKS)]
+        offsets = held.tile([P, NEIGHBOURS * PIECE_COLS], U16, name="offsets")
+        bias = held.tile([P, M_BLOCKS], F32, name="bias")
+
+        nc.sync.dma_start(table_blocks[0][:], table[0:P, :])
+        nc.scalar.dma_start(w_blocks[0][:], w[0:P, :])
+        nc.sync.dma_start(offsets[:], offs)
+        nc.scalar.dma_start(table_blocks[1][:], table[P : 2 * P, :])
+        nc.sync.dma_start(w_blocks[1][:], w[P : 2 * P, :])
+        nc.sync.dma_start(bias[:], b.rearrange("(a p) o -> p (a o)", p=P))
+
+        for mb in range(M_BLOCKS):
+            bank = psum.tile([P, V], F32, name="bank%d" % mb)
+            passes = [(kb, t) for kb in range(K_BLOCKS) for t in range(NEIGHBOURS)]
+            for i, (kb, t) in enumerate(passes):
+                piece = offsets[:, t * PIECE_COLS : (t + 1) * PIECE_COLS]
+                nc.tensor.matmul(
+                    bank[:],
+                    w_blocks[kb][:, mb * P : (mb + 1) * P],
+                    table_blocks[kb][:].indirect(piece),
+                    start=(i == 0),
+                    stop=(i == len(passes) - 1),
+                )
+            result = held.tile([P, V], F32, name="result%d" % mb)
+            nc.vector.tensor_scalar(
+                result[:],
+                bank[:],
+                bias[:, mb : mb + 1],
+                0.0,
+                mybir.AluOpType.add,
+                mybir.AluOpType.max,
+            )
+            nc.sync.dma_start(out[mb * P : (mb + 1) * P, :], result[:])

@@ -33,7 +33,8 @@ def tile_gather_matmul_kernel(tc, table, w, b, offs, out):
         nc.sync.dma_start(offsets[:], offs)
         nc.scalar.dma_start(table_blocks[1][:], table[P : 2 * P, :])
         nc.sync.dma_start(w_blocks[1][:], w[P : 2 * P, :])
-        nc.sync.dma_start(bias[:], b.rearrange("(a p) o -> p (a o)", p=P))
+        nc.sync.dma_start(bias[:], b.rearrange("(p a) o -> p (a o)", a=M_BLOCKS))
+        out_blocks = out.rearrange("(p a) v -> p a v", a=M_BLOCKS)
 
         for mb in range(M_BLOCKS):
             bank = psum.tile([P, V], F32, name="bank%d" % mb)
@@ -42,7 +43,7 @@ def tile_gather_matmul_kernel(tc, table, w, b, offs, out):
                 piece = offsets[:, t * PIECE_COLS : (t + 1) * PIECE_COLS]
                 nc.tensor.matmul(
                     bank[:],
-                    w_blocks[kb][:, mb * P : (mb + 1) * P],
+                    w_blocks[kb][:, mb::M_BLOCKS],
                     table_blocks[kb][:].indirect(piece),
                     start=(i == 0),
                     stop=(i == len(passes) - 1),
@@ -56,4 +57,4 @@ def tile_gather_matmul_kernel(tc, table, w, b, offs, out):
                 mybir.AluOpType.add,
                 mybir.AluOpType.max,
             )
-            nc.sync.dma_start(out[mb * P : (mb + 1) * P, :], result[:])
+            nc.sync.dma_start(out_blocks[:, mb, :], result[:])

import concourse.mybir as mybir

P = 128
K = 256
M = 256
S = 512
V = 192
NEIGHBOURS = 2
K_BLOCKS = K // P
M_BLOCKS = M // P
PIECE_COLS = V // 16

FLOPS = 2 * K * M * V

BF16 = mybir.dt.bfloat16
F32 = mybir.dt.float32
U16 = mybir.dt.uint16


def tile_gather_matmul_kernel(tc, table, w, b, offs, out):
    nc = tc.nc
    with (
        tc.tile_pool(name="held", bufs=1) as held,
        tc.psum_pool(name="psum", bufs=1) as psum,
    ):
        table_blocks = [held.tile([P, S], BF16, name="table_block%d" % kb) for kb in range(K_BLOCKS)]
        w_blocks = [held.tile([P, M], BF16, name="w_block%d" % kb) for kb in range(K_BLOCKS)]
        offsets = held.tile([P, NEIGHBOURS * PIECE_COLS], U16, name="offsets")
        bias = held.tile([P, M_BLOCKS], F32, name="bias")

        nc.sync.dma_start(table_blocks[0][:], table[0:P, :])
        nc.scalar.dma_start(w_blocks[0][:], w[0:P, :])
        nc.sync.dma_start(offsets[:], offs)
        nc.scalar.dma_start(table_blocks[1][:], table[P : 2 * P, :])
        nc.sync.dma_start(w_blocks[1][:], w[P : 2 * P, :])
        nc.sync.dma_start(bias[:], b.rearrange("(p a) o -> p (a o)", a=M_BLOCKS))
        out_blocks = out.rearrange("(p a) v -> p a v", a=M_BLOCKS)

        for mb in range(M_BLOCKS):
            bank = psum.tile([P, V], F32, name="bank%d" % mb)
            passes = [(kb, t) for kb in range(K_BLOCKS) for t in range(NEIGHBOURS)]
            for i, (kb, t) in enumerate(passes):
                piece = offsets[:, t * PIECE_COLS : (t + 1) * PIECE_COLS]
                nc.tensor.matmul(
                    bank[:],
                    w_blocks[kb][:, mb::M_BLOCKS],
                    table_blocks[kb][:].indirect(piece),
                    start=(i == 0),
                    stop=(i == len(passes) - 1),
                )
            result = held.tile([P, V], F32, name="result%d" % mb)
            nc.vector.tensor_scalar(
                result[:],
                bank[:],
                bias[:, mb : mb + 1],
                0.0,
                mybir.AluOpType.add,
                mybir.AluOpType.max,
            )
            nc.sync.dma_start(out_blocks[:, mb, :], result[:])
